import numpy as np
import ml_dtypes


def mxq(x, axis, fmt="e4m3"):
    dtype, down = {"e4m3": (ml_dtypes.float8_e4m3fn, 7), "e5m2": (ml_dtypes.float8_e5m2, 14)}[fmt]
    v = np.moveaxis(np.asarray(x, np.float32).astype(ml_dtypes.bfloat16).astype(np.float64), axis, -1)
    blocks = v.reshape(v.shape[:-1] + (-1, 32))
    amax = np.abs(blocks).max(-1, keepdims=True)
    byte = np.maximum(np.where(amax > 0, np.frexp(amax)[1] - 1 + 127, 0) - down, 1)
    scale = np.exp2(byte - 127.0)
    codes = (blocks / scale).astype(np.float32).astype(dtype).astype(np.float64)
    return np.moveaxis((codes * scale).reshape(v.shape), -1, axis)


WIDE = False


def mx_kscale(k):
    if not WIDE:
        return np.ones(k)
    levels = np.array([10, -10, 5, -5, 0])
    if k % 512:
        return np.exp2(np.random.permutation(np.resize(levels, k // 32))).repeat(32)
    a = np.empty((k // 512, 16))
    for p in range(k // 512):
        a[p, :8] = np.random.permutation(np.resize(levels, 8))
        for g in range(8):
            far = levels[np.abs(levels - a[p, g]) >= 10]
            a[p, g + 8] = far[np.random.randint(len(far))]
    return np.exp2(a.ravel()).repeat(32)


def f64(x):
    return np.asarray(x).astype(np.float64)


def striped(idx):
    return np.tile(np.asarray(idx).reshape(-1, 16).T, (8, 1)).astype(np.uint16)


def unstriped(offs):
    return offs[:16].T.reshape(-1).astype(np.int64)


E2M1 = np.array([0.0, 0.5, 1.0, 1.5, 2.0, 3.0, 4.0, 6.0, -0.0, -0.5, -1.0, -1.5, -2.0, -3.0, -4.0, -6.0])


def pack_weight(w, fmt):
    k, n = w.shape
    w = f64(np.asarray(w, np.float32).astype(ml_dtypes.bfloat16)).reshape(k // 32, 32, n)
    amax = np.abs(w).max(1)
    if fmt == "e4m3":
        byte = np.frexp(amax)[1] - 1 + 127 - 7
    else:
        mant, ex = np.frexp(amax / 6.0)
        byte = np.where(mant > 0.5, ex, ex - 1) + 127
    byte = np.clip(np.where(amax > 0, byte, 1), 1, 254)
    scaled = (w * np.exp2(127.0 - byte)[:, None, :]).reshape(k, n).astype(np.float32)
    by_word = np.ascontiguousarray(scaled.reshape(k // 512, 128, 4, n).transpose(0, 1, 3, 2))
    if fmt == "e4m3":
        words = by_word.astype(ml_dtypes.float8_e4m3fn).view(np.uint8)
    else:
        c = by_word.astype(ml_dtypes.float4_e2m1fn).view(np.uint8) & 0xF
        words = (c[..., 0::2] | (c[..., 1::2] << 4)).reshape(k // 512, 128, 2 * n)
    return np.ascontiguousarray(words), np.ascontiguousarray(byte.astype(np.uint8).reshape(k // 512, 16, n))


def unpack_weight(words, scales, fmt):
    g, _, n = scales.shape
    words = np.ascontiguousarray(words).reshape(g, 128, n, -1)
    if fmt == "e4m3":
        vals = words.view(ml_dtypes.float8_e4m3fn).astype(np.float64)
    else:
        nib = np.empty((g, 128, n, 4), np.uint8)
        nib[..., 0::2] = words & 0xF
        nib[..., 1::2] = words >> 4
        vals = E2M1[nib]
    vals = vals * np.repeat(np.exp2(scales.astype(np.float64) - 127.0), 8, axis=1)[..., None]
    return vals.transpose(0, 1, 3, 2).reshape(g * 512, n)


def bf(x):
    return np.asarray(x, np.float32).astype(ml_dtypes.bfloat16)


def planes(Y):
    r, m = Y.shape
    b = f64(bf(Y)).reshape(r // 32, 32, m)
    amax = np.abs(b).max(1)
    byte = np.clip(np.where(amax > 0, np.frexp(amax)[1] - 1 + 127 - 7, 1), 1, 254)
    codes = (b * np.exp2(127.0 - byte)[:, None, :]).reshape(r, m).astype(np.float32).astype(ml_dtypes.float8_e4m3fn).view(np.uint8)
    words = codes.reshape(r // 512, 128, 4, m).transpose(0, 1, 3, 2)
    return np.ascontiguousarray(words), np.ascontiguousarray(byte.astype(np.uint8).reshape(r // 512, 16, m))


D, E, T, I, Q = 512, 512, 2048, 512, 256


def setup_inputs():
    n = np.random.standard_normal
    idx = np.random.permutation(T)[:I]
    fd = mx_kscale(D)
    fi = mx_kscale(I)
    ti = np.ones(T)
    ti[idx] = fi
    keysp = pack_weight(n((D, T)) / fd[:, None], "e4m3")
    return {
        "query": (n((D, Q)) * 1.0 / np.sqrt(D) * fd[:, None]).astype(np.float32),
        "keys_words": keysp[0],
        "keys_scales": keysp[1],
        "sharp": (np.random.uniform(0.4, 1.0, (Q, 1))).astype(np.float32),
        "os": (np.random.uniform(4.0, 16.0, (1, I)) * fi).astype(np.float32),
        "vals": (n((E, T)) / ti).astype(np.float32),
        "offs": striped(idx),
    }


def reference(query, keys_words, keys_scales, sharp, os, vals, offs):
    idx = unstriped(offs)
    keysu = unpack_weight(keys_words, keys_scales, "e4m3")
    queryq = mxq(f64(query), 0, "e4m3")
    keysidxg = keysu[:, idx]
    a = queryq.T @ keysidxg
    m1 = np.mean(a, axis=1, keepdims=True)
    ce = a - m1
    sd = np.sqrt(np.mean(np.square(ce), axis=1, keepdims=True) + 0.05)
    s = ce / sd * f64(sharp)
    p = np.exp(s - np.max(s, axis=1, keepdims=True))
    z = np.sum(p, axis=1, keepdims=True)
    w = p / z
    wo1 = w * f64(os)
    wt1 = wo1.T
    vt1 = f64(vals)[:, idx].T
    vt1q = mxq(vt1, 0, "e4m3")
    wt1q = mxq(wt1, 0, "e4m3")
    o = vt1q.T @ wt1q
    words, scales = planes(o)
    return o, words, scales

@@ -1,0 +1,200 @@
+from contextlib import ExitStack
+
+import concourse.mybir as mybir
+from concourse.masks import make_identity
+
+D, E, T, I, Q = 512, 512, 2048, 512, 256
+FLOPS = 2 * Q * I * D + 2 * E * I * Q
+
+F32 = mybir.dt.float32
+BF16 = mybir.dt.bfloat16
+I32 = mybir.dt.int32
+U32 = mybir.dt.uint32
+U16 = mybir.dt.uint16
+U8 = mybir.dt.uint8
+FP8X4 = mybir.dt.float8_e4m3fn_x4
+ALU = mybir.AluOpType
+ACT = mybir.ActivationFunctionType
+
+P = 128
+PACK = 4
+HALVES = Q // P
+EPS = 0.05
+REUSED = ("q_bf1", "largest", "sharpened1", "weights1")
+VECTOR_COLS = (0, 32, 0, 18)
+
+
+def tile_attend_standardised_pl_kernel(tc, query, keys_words, keys_scales, sharp, slot_factor, vals, offs, out_0, out_1, out_2):
+    nc = tc.nc
+    with ExitStack() as ctx:
+        keep = ctx.enter_context(tc.tile_pool(name="keep", bufs=1))
+        psum = ctx.enter_context(tc.psum_pool(name="psum", bufs=1))
+
+        def sb(name, shape, dtype, tag=None):
+            return keep.tile(shape, dtype, name=name, tag=tag or name, align_bytes=64)
+
+        offsets = keep.tile([P, I // 16], U16, name="offsets")
+        key_bytes = sb("key_bytes", [P, T], U8)
+        nc.gpsimd.memset(key_bytes[:].bitcast(I32), 0)
+        q_raw = sb("q_raw", [P, PACK, Q], F32)
+        scale_rows = keys_scales[0].bitcast(I32)
+        key_words = sb("key_words", [P, T], U32)
+        sharp_sb = sb("sharp_sb", [P, HALVES], F32)
+        factor_cols = sb("factor_cols", [P, PACK], F32)
+        val_planes = vals.rearrange("(p t) c -> p t c", t=PACK)
+        val_pool = [sb("val_pool%d" % t, [P, T], F32) for t in range(PACK)]
+        nc.sync.dma_start(offsets[:], offs)
+        nc.sync.dma_start(key_words[:].bitcast(I32), keys_words[0].rearrange("p n t -> p (n t)").bitcast(I32))
+        for quad in range(4):
+            nc.sync.dma_start(key_bytes[32 * quad : 32 * quad + 4, :].bitcast(I32), scale_rows[4 * quad : 4 * quad + 4, :])
+        nc.sync.dma_start(q_raw[:], query.rearrange("(p j) q -> p j q", j=PACK))
+        nc.sync.dma_start(factor_cols[:], slot_factor[0].rearrange("(s r) -> s r", r=PACK))
+        nc.sync.dma_start(val_pool[0][:], val_planes[:, 0, :])
+        with nc.allow_non_contiguous_dma(reason="one value a query row"):
+            nc.sync.dma_start(sharp_sb[:], sharp.rearrange("(h p) o -> p (h o)", p=P))
+        nc.sync.dma_start(val_pool[1][:], val_planes[:, 1, :])
+        nc.sync.dma_start(val_pool[2][:], val_planes[:, 2, :])
+        nc.sync.dma_start(val_pool[3][:], val_planes[:, 3, :])
+
+        ident = sb("ident", [P, P], F32)
+        make_identity(nc, ident[:])
+        minus_half = sb("minus_half", [P, HALVES], F32)
+        nc.gpsimd.memset(minus_half[:], -0.5)
+
+        factor_rows = psum.tile([P, PACK, P], F32, name="factor_rows")
+        for r in range(PACK):
+            nc.tensor.transpose(factor_rows[:, r, :], factor_cols[:, r : r + 1].to_broadcast([P, P]), ident[:])
+
+        picked_bytes = sb("picked_bytes", [P, I], U8)
+        nc.vector.tensor_copy(picked_bytes[:], key_bytes[:].indirect(offsets[:]))
+        picked_words = sb("picked_words", [P, I], U32)
+        nc.vector.tensor_copy(picked_words[:], key_words[:].indirect(offsets[:]))
+        scores = []
+        for h in range(HALVES):
+            cols = slice(h * P, (h + 1) * P)
+            q_bf = sb("q_bf%d" % h, [P, P, PACK], BF16)
+            interleave = nc.scalar.copy
+            interleave(q_bf[:].rearrange("p (c i) t -> p c t i", i=4), q_raw[:, :, cols].rearrange("p t (c i) -> p c t i", i=4))
+            q_codes = sb("q_codes%d" % h, [P, P], U32)
+            q_scales = sb("q_scales%d" % h, [P, P], U8)
+            nc.vector.quantize_mx(out=q_codes[:].bitcast(FP8X4), scales=q_scales[:], in_=q_bf[:].rearrange("p q t -> p (q t)"))
+            bank = psum.tile([P, I], F32, name="scores%d" % h, tag="half%d" % h)
+            nc.tensor.matmul_mx(out=bank[:], lhsT=q_codes[:].bitcast(FP8X4), lhsT_scale=q_scales[:],
+                                rhs=picked_words[:].bitcast(FP8X4), rhs_scale=picked_bytes[:], start=True, stop=True)
+            scores.append(bank)
+
+        def turn_pairs(rows, turned):
+            words = rows[:].bitcast(F32)
+            for u in range(2):
+                nc.tensor.transpose(turned[:, u, :], words[:, u : I // 2 : 2], ident[:])
+
+        def quantise_turned(name, turned, copy, tag=None):
+            grouped = sb(name + "_grouped", [P, P, 2], F32)
+            copy(grouped[:], turned[:].rearrange("p u c -> p c u"))
+            codes = sb(name + "_codes", [P, P], U32, tag=tag)
+            scales = sb(name + "_scales", [P, P], U8)
+            nc.vector.quantize_mx(out=codes[:].bitcast(FP8X4), scales=scales[:],
+                                  in_=grouped[:].rearrange("p c u -> p (c u)").bitcast(BF16))
+            return codes, scales
+
+        def gather_values(t):
+            picked = sb("picked_vals%d" % t, [P, I], BF16, tag=REUSED[t])
+            c = VECTOR_COLS[t]
+            if c:
+                nc.vector.tensor_copy(picked[:, : 16 * c], val_pool[t][:].indirect(offsets[:, :c]))
+            if c < I // 16:
+                nc.scalar.activation(picked[:, 16 * c :], val_pool[t][:].indirect(offsets[:, c:]), ACT.Copy)
+            turned = psum.tile([P, 2, P], F32, name="val_turned%d" % t, tag="val%d" % (t % 2))
+            turn_pairs(picked, turned)
+            return turned
+
+        def exponentials():
+            stats = sb("stats", [P, HALVES, 6], F32)
+            mean_var = sb("mean_var", [P, HALVES, 2], F32)
+            for h in range(HALVES):
+                nc.vector.bn_stats(stats[:, h, :], scores[h][:])
+            for h in range(HALVES):
+                nc.vector.bn_aggr(mean_var[:, h, :], stats[:, h, :])
+            spread_sq = sb("spread_sq", [P, HALVES], F32)
+            nc.vector.tensor_scalar(spread_sq[:], mean_var[:, :, 1], EPS, None, ALU.add)
+            inv_spread = sb("inv_spread", [P, HALVES], F32)
+            nc.gpsimd.tensor_tensor(inv_spread[:], spread_sq[:], minus_half[:], ALU.pow)
+            sharpened = [sb("sharpened%d" % h, [P, I], F32) for h in range(HALVES)]
+            largest = sb("largest", [P, HALVES], F32)
+            for h in range(HALVES):
+                nc.vector.tensor_scalar(sharpened[h][:], scores[h][:], sharp_sb[:, h : h + 1], None, ALU.mult, ALU.max,
+                                        accum_out=largest[:, h : h + 1])
+            shift = sb("shift", [P, HALVES], F32)
+            nc.vector.scalar_tensor_tensor(shift[:], largest[:], -1.0, inv_spread[:], ALU.mult, ALU.mult)
+            made = []
+            for h in range(HALVES):
+                probs = sb("probs%d" % h, [P, I], F32)
+                total = sb("total%d" % h, [P, 1], F32)
+                nc.scalar.activation(probs[:], sharpened[h][:], ACT.Exp, bias=shift[:, h : h + 1],
+                                     scale=inv_spread[:, h : h + 1], accum_out=total[:])
+                made.append((probs, total))
+            return made
+
+        def turned_weights(h, probs, total):
+            inv_total = sb("inv_total%d" % h, [P, 1], F32)
+            nc.vector.reciprocal(inv_total[:], total[:])
+            weights = sb("weights%d" % h, [P, I], BF16)
+            nc.vector.scalar_tensor_tensor(weights[:].rearrange("p (s r) -> p s r", r=PACK),
+                                           probs[:].rearrange("p (s r) -> p s r", r=PACK), inv_total[:],
+                                           factor_rows[:].rearrange("p r s -> p s r"), ALU.mult, ALU.mult)
+            turned = psum.tile([P, 2, P], F32, name="w_turned%d" % h, tag="half%d" % h)
+            turn_pairs(weights, turned)
+            return turned
+
+        V, S = nc.vector.tensor_copy, nc.scalar.copy
+        vq, wq = {}, {}
+        e0, e1 = exponentials()
+        vt0 = gather_values(0)
+        vt1 = gather_values(1)
+        wt0 = turned_weights(0, *e0)
+        wt1 = turned_weights(1, *e1)
+        vq[0] = quantise_turned("val0", vt0, S, tag="spread_sq")
+        vq[1] = quantise_turned("val1", vt1, V)
+        vt2 = gather_values(2)
+        w_grouped = sb("w_grouped", [P, Q, 2], F32)
+        V(w_grouped[:, :P, :], wt0[:].rearrange("p u c -> p c u"))
+        S(w_grouped[:, P:, :], wt1[:].rearrange("p u c -> p c u"))
+        w_codes = sb("w_codes", [P, Q], U32)
+        w_scales = sb("w_scales", [P, Q], U8)
+        nc.vector.quantize_mx(out=w_codes[:].bitcast(FP8X4), scales=w_scales[:],
+                              in_=w_grouped[:].rearrange("p c u -> p (c u)").bitcast(BF16))
+        vq[2] = quantise_turned("val2", vt2, S)
+
+        out_planes = out_0.rearrange("(p t) q -> p t q", t=PACK)
+        last = PACK - 1
+        pair_sums = psum.tile([P, 2, Q], F32, name="pair_sums")
+        sums = [pair_sums[:, 0, :], pair_sums[:, 1, :]] + [psum.tile([P, Q], F32, name="sums%d" % t)[:] for t in (2, 3)]
+
+        def multiply(t):
+            nc.tensor.matmul_mx(out=sums[t], lhsT=vq[t][0][:].bitcast(FP8X4), lhsT_scale=vq[t][1][:],
+                                rhs=w_codes[:].bitcast(FP8X4), rhs_scale=w_scales[:], start=True, stop=True)
+
+        y = sb("y", [P, PACK, Q], F32)
+        vt3 = gather_values(last)
+        for t in range(last):
+            multiply(t)
+        vq[last] = quantise_turned("val3", vt3, V)
+        nc.scalar.copy(y[:, :2, :], pair_sums[:])
+        nc.scalar.copy(y[:, 2, :], sums[2])
+        nc.sync.dma_start(out_planes[:, :last, :], y[:, :last, :])
+        multiply(last)
+        nc.vector.tensor_copy(y[:, last, :], sums[last])
+        nc.sync.dma_start(out_planes[:, last, :], y[:, last, :])
+
+        y_bf = sb("y_bf", [P, Q, PACK], BF16)
+        split = 160
+        for copy, cols in ((V, slice(0, split)), (S, slice(split, Q))):
+            copy(y_bf[:, cols, :].rearrange("p (c i) t -> p c t i", i=4), y[:, :, cols].rearrange("p t (c i) -> p c t i", i=4))
+        y_codes = sb("y_codes", [P, Q], U32)
+        y_scales = sb("y_scales", [P, Q], U8)
+        nc.vector.quantize_mx(out=y_codes[:].bitcast(FP8X4), scales=y_scales[:], in_=y_bf[:].rearrange("p q t -> p (q t)"))
+        nc.sync.dma_start(out_1[0].rearrange("p n t -> p (n t)").bitcast(I32), y_codes[:].bitcast(I32))
+        out_rows = out_2[0].bitcast(I32)
+        for quad in range(4):
+            queue = nc.sync if quad < 2 else nc.scalar
+            queue.dma_start(out_rows[4 * quad : 4 * quad + 4, :], y_scales[32 * quad : 32 * quad + 4, :].bitcast(I32))

@@ -20,8 +20,8 @@ P = 128
 PACK = 4
 HALVES = Q // P
 EPS = 0.05
-REUSED = ("q_bf1", "largest", "sharpened1", "weights1")
-VECTOR_COLS = (0, 32, 0, 18)
+REUSED = ("q_bf1", None, "sharpened1", "probs1")
+VECTOR_COLS = (0, 0, 0, 32)
 
 
 def tile_attend_standardised_pl_kernel(tc, query, keys_words, keys_scales, sharp, slot_factor, vals, offs, out_0, out_1, out_2):
@@ -45,10 +45,10 @@ def tile_attend_standardised_pl_kernel(tc, query, keys_words, keys_scales, sharp
         val_pool = [sb("val_pool%d" % t, [P, T], F32) for t in range(PACK)]
         nc.sync.dma_start(offsets[:], offs)
         nc.sync.dma_start(key_words[:].bitcast(I32), keys_words[0].rearrange("p n t -> p (n t)").bitcast(I32))
+        nc.sync.dma_start(factor_cols[:], slot_factor[0].rearrange("(s r) -> s r", r=PACK))
         for quad in range(4):
             nc.sync.dma_start(key_bytes[32 * quad : 32 * quad + 4, :].bitcast(I32), scale_rows[4 * quad : 4 * quad + 4, :])
         nc.sync.dma_start(q_raw[:], query.rearrange("(p j) q -> p j q", j=PACK))
-        nc.sync.dma_start(factor_cols[:], slot_factor[0].rearrange("(s r) -> s r", r=PACK))
         nc.sync.dma_start(val_pool[0][:], val_planes[:, 0, :])
         with nc.allow_non_contiguous_dma(reason="one value a query row"):
             nc.sync.dma_start(sharp_sb[:], sharp.rearrange("(h p) o -> p (h o)", p=P))
@@ -88,12 +88,13 @@ def tile_attend_standardised_pl_kernel(tc, query, keys_words, keys_scales, sharp
             for u in range(2):
                 nc.tensor.transpose(turned[:, u, :], words[:, u : I // 2 : 2], ident[:])
 
-        def quantise_turned(name, turned, copy, tag=None):
-            grouped = sb(name + "_grouped", [P, P, 2], F32)
+        def quantise_turned(name, turned, copy, tag=None, codes_tag=None, codes=None):
+            grouped = sb(name + "_grouped", [P, P, 2], F32, tag=tag)
             copy(grouped[:], turned[:].rearrange("p u c -> p c u"))
-            codes = sb(name + "_codes", [P, P], U32, tag=tag)
+            if codes is None:
+                codes = sb(name + "_codes", [P, P], U32, tag=codes_tag)[:]
             scales = sb(name + "_scales", [P, P], U8)
-            nc.vector.quantize_mx(out=codes[:].bitcast(FP8X4), scales=scales[:],
+            nc.vector.quantize_mx(out=codes.bitcast(FP8X4), scales=scales[:],
                                   in_=grouped[:].rearrange("p c u -> p (c u)").bitcast(BF16))
             return codes, scales
 
@@ -148,22 +149,24 @@ def tile_attend_standardised_pl_kernel(tc, query, keys_words, keys_scales, sharp
 
         V, S = nc.vector.tensor_copy, nc.scalar.copy
         vq, wq = {}, {}
-        e0, e1 = exponentials()
         vt0 = gather_values(0)
         vt1 = gather_values(1)
+        e0, e1 = exponentials()
+        vq[0] = quantise_turned("val0", vt0, V, tag="sharp_sb")
         wt0 = turned_weights(0, *e0)
         wt1 = turned_weights(1, *e1)
-        vq[0] = quantise_turned("val0", vt0, S, tag="spread_sq")
-        vq[1] = quantise_turned("val1", vt1, V)
+        vq[1] = quantise_turned("val1", vt1, V, tag="largest", codes_tag="total1")
         vt2 = gather_values(2)
         w_grouped = sb("w_grouped", [P, Q, 2], F32)
-        V(w_grouped[:, :P, :], wt0[:].rearrange("p u c -> p c u"))
+        S(w_grouped[:, :P, :], wt0[:].rearrange("p u c -> p c u"))
+        vt3 = gather_values(3)
         S(w_grouped[:, P:, :], wt1[:].rearrange("p u c -> p c u"))
-        w_codes = sb("w_codes", [P, Q], U32)
+        late_codes = sb("late_codes", [P, Q + P], U32, tag="val_pool3")
+        w_codes = late_codes[:, :Q]
         w_scales = sb("w_scales", [P, Q], U8)
-        nc.vector.quantize_mx(out=w_codes[:].bitcast(FP8X4), scales=w_scales[:],
+        nc.vector.quantize_mx(out=w_codes.bitcast(FP8X4), scales=w_scales[:],
                               in_=w_grouped[:].rearrange("p c u -> p (c u)").bitcast(BF16))
-        vq[2] = quantise_turned("val2", vt2, S)
+        vq[2] = quantise_turned("val2", vt2, S, codes=late_codes[:, Q:])
 
         out_planes = out_0.rearrange("(p t) q -> p t q", t=PACK)
         last = PACK - 1
@@ -171,11 +174,10 @@ def tile_attend_standardised_pl_kernel(tc, query, keys_words, keys_scales, sharp
         sums = [pair_sums[:, 0, :], pair_sums[:, 1, :]] + [psum.tile([P, Q], F32, name="sums%d" % t)[:] for t in (2, 3)]
 
         def multiply(t):
-            nc.tensor.matmul_mx(out=sums[t], lhsT=vq[t][0][:].bitcast(FP8X4), lhsT_scale=vq[t][1][:],
-                                rhs=w_codes[:].bitcast(FP8X4), rhs_scale=w_scales[:], start=True, stop=True)
+            nc.tensor.matmul_mx(out=sums[t], lhsT=vq[t][0].bitcast(FP8X4), lhsT_scale=vq[t][1][:],
+                                rhs=w_codes.bitcast(FP8X4), rhs_scale=w_scales[:], start=True, stop=True)
 
         y = sb("y", [P, PACK, Q], F32)
-        vt3 = gather_values(last)
         for t in range(last):
             multiply(t)
         vq[last] = quantise_turned("val3", vt3, V)

from contextlib import ExitStack

import concourse.mybir as mybir
from concourse.masks import make_identity

D, E, T, I, Q = 512, 512, 2048, 512, 256
FLOPS = 2 * Q * I * D + 2 * E * I * Q

F32 = mybir.dt.float32
BF16 = mybir.dt.bfloat16
I32 = mybir.dt.int32
U32 = mybir.dt.uint32
U16 = mybir.dt.uint16
U8 = mybir.dt.uint8
FP8X4 = mybir.dt.float8_e4m3fn_x4
ALU = mybir.AluOpType
ACT = mybir.ActivationFunctionType

P = 128
PACK = 4
HALVES = Q // P
EPS = 0.05
REUSED = ("q_bf1", None, "sharpened1", "probs1")
VECTOR_COLS = (0, 0, 0, 32)


def tile_attend_standardised_pl_kernel(tc, query, keys_words, keys_scales, sharp, slot_factor, vals, offs, out_0, out_1, out_2):
    nc = tc.nc
    with ExitStack() as ctx:
        keep = ctx.enter_context(tc.tile_pool(name="keep", bufs=1))
        psum = ctx.enter_context(tc.psum_pool(name="psum", bufs=1))

        def sb(name, shape, dtype, tag=None):
            return keep.tile(shape, dtype, name=name, tag=tag or name, align_bytes=64)

        offsets = keep.tile([P, I // 16], U16, name="offsets")
        key_bytes = sb("key_bytes", [P, T], U8)
        nc.gpsimd.memset(key_bytes[:].bitcast(I32), 0)
        q_raw = sb("q_raw", [P, PACK, Q], F32)
        scale_rows = keys_scales[0].bitcast(I32)
        key_words = sb("key_words", [P, T], U32)
        sharp_sb = sb("sharp_sb", [P, HALVES], F32)
        factor_cols = sb("factor_cols", [P, PACK], F32)
        val_planes = vals.rearrange("(p t) c -> p t c", t=PACK)
        val_pool = [sb("val_pool%d" % t, [P, T], F32) for t in range(PACK)]
        nc.sync.dma_start(offsets[:], offs)
        nc.sync.dma_start(key_words[:].bitcast(I32), keys_words[0].rearrange("p n t -> p (n t)").bitcast(I32))
        nc.sync.dma_start(factor_cols[:], slot_factor[0].rearrange("(s r) -> s r", r=PACK))
        for quad in range(4):
            nc.sync.dma_start(key_bytes[32 * quad : 32 * quad + 4, :].bitcast(I32), scale_rows[4 * quad : 4 * quad + 4, :])
        nc.sync.dma_start(q_raw[:], query.rearrange("(p j) q -> p j q", j=PACK))
        nc.sync.dma_start(val_pool[0][:], val_planes[:, 0, :])
        with nc.allow_non_contiguous_dma(reason="one value a query row"):
            nc.sync.dma_start(sharp_sb[:], sharp.rearrange("(h p) o -> p (h o)", p=P))
        nc.sync.dma_start(val_pool[1][:], val_planes[:, 1, :])
        nc.sync.dma_start(val_pool[2][:], val_planes[:, 2, :])
        nc.sync.dma_start(val_pool[3][:], val_planes[:, 3, :])

        ident = sb("ident", [P, P], F32)
        make_identity(nc, ident[:])
        minus_half = sb("minus_half", [P, HALVES], F32)
        nc.gpsimd.memset(minus_half[:], -0.5)

        factor_rows = psum.tile([P, PACK, P], F32, name="factor_rows")
        for r in range(PACK):
            nc.tensor.transpose(factor_rows[:, r, :], factor_cols[:, r : r + 1].to_broadcast([P, P]), ident[:])

        picked_bytes = sb("picked_bytes", [P, I], U8)
        nc.vector.tensor_copy(picked_bytes[:], key_bytes[:].indirect(offsets[:]))
        picked_words = sb("picked_words", [P, I], U32)
        nc.vector.tensor_copy(picked_words[:], key_words[:].indirect(offsets[:]))
        scores = []
        for h in range(HALVES):
            cols = slice(h * P, (h + 1) * P)
            q_bf = sb("q_bf%d" % h, [P, P, PACK], BF16)
            interleave = nc.scalar.copy
            interleave(q_bf[:].rearrange("p (c i) t -> p c t i", i=4), q_raw[:, :, cols].rearrange("p t (c i) -> p c t i", i=4))
            q_codes = sb("q_codes%d" % h, [P, P], U32)
            q_scales = sb("q_scales%d" % h, [P, P], U8)
            nc.vector.quantize_mx(out=q_codes[:].bitcast(FP8X4), scales=q_scales[:], in_=q_bf[:].rearrange("p q t -> p (q t)"))
            bank = psum.tile([P, I], F32, name="scores%d" % h, tag="half%d" % h)
            nc.tensor.matmul_mx(out=bank[:], lhsT=q_codes[:].bitcast(FP8X4), lhsT_scale=q_scales[:],
                                rhs=picked_words[:].bitcast(FP8X4), rhs_scale=picked_bytes[:], start=True, stop=True)
            scores.append(bank)

        def turn_pairs(rows, turned):
            words = rows[:].bitcast(F32)
            for u in range(2):
                nc.tensor.transpose(turned[:, u, :], words[:, u : I // 2 : 2], ident[:])

        def quantise_turned(name, turned, copy, tag=None, codes_tag=None, codes=None):
            grouped = sb(name + "_grouped", [P, P, 2], F32, tag=tag)
            copy(grouped[:], turned[:].rearrange("p u c -> p c u"))
            if codes is None:
                codes = sb(name + "_codes", [P, P], U32, tag=codes_tag)[:]
            scales = sb(name + "_scales", [P, P], U8)
            nc.vector.quantize_mx(out=codes.bitcast(FP8X4), scales=scales[:],
                                  in_=grouped[:].rearrange("p c u -> p (c u)").bitcast(BF16))
            return codes, scales

        def gather_values(t):
            picked = sb("picked_vals%d" % t, [P, I], BF16, tag=REUSED[t])
            c = VECTOR_COLS[t]
            if c:
                nc.vector.tensor_copy(picked[:, : 16 * c], val_pool[t][:].indirect(offsets[:, :c]))
            if c < I // 16:
                nc.scalar.activation(picked[:, 16 * c :], val_pool[t][:].indirect(offsets[:, c:]), ACT.Copy)
            turned = psum.tile([P, 2, P], F32, name="val_turned%d" % t, tag="val%d" % (t % 2))
            turn_pairs(picked, turned)
            return turned

        def exponentials():
            stats = sb("stats", [P, HALVES, 6], F32)
            mean_var = sb("mean_var", [P, HALVES, 2], F32)
            for h in range(HALVES):
                nc.vector.bn_stats(stats[:, h, :], scores[h][:])
            for h in range(HALVES):
                nc.vector.bn_aggr(mean_var[:, h, :], stats[:, h, :])
            spread_sq = sb("spread_sq", [P, HALVES], F32)
            nc.vector.tensor_scalar(spread_sq[:], mean_var[:, :, 1], EPS, None, ALU.add)
            inv_spread = sb("inv_spread", [P, HALVES], F32)
            nc.gpsimd.tensor_tensor(inv_spread[:], spread_sq[:], minus_half[:], ALU.pow)
            sharpened = [sb("sharpened%d" % h, [P, I], F32) for h in range(HALVES)]
            largest = sb("largest", [P, HALVES], F32)
            for h in range(HALVES):
                nc.vector.tensor_scalar(sharpened[h][:], scores[h][:], sharp_sb[:, h : h + 1], None, ALU.mult, ALU.max,
                                        accum_out=largest[:, h : h + 1])
            shift = sb("shift", [P, HALVES], F32)
            nc.vector.scalar_tensor_tensor(shift[:], largest[:], -1.0, inv_spread[:], ALU.mult, ALU.mult)
            made = []
            for h in range(HALVES):
                probs = sb("probs%d" % h, [P, I], F32)
                total = sb("total%d" % h, [P, 1], F32)
                nc.scalar.activation(probs[:], sharpened[h][:], ACT.Exp, bias=shift[:, h : h + 1],
                                     scale=inv_spread[:, h : h + 1], accum_out=total[:])
                made.append((probs, total))
            return made

        def turned_weights(h, probs, total):
            inv_total = sb("inv_total%d" % h, [P, 1], F32)
            nc.vector.reciprocal(inv_total[:], total[:])
            weights = sb("weights%d" % h, [P, I], BF16)
            nc.vector.scalar_tensor_tensor(weights[:].rearrange("p (s r) -> p s r", r=PACK),
                                           probs[:].rearrange("p (s r) -> p s r", r=PACK), inv_total[:],
                                           factor_rows[:].rearrange("p r s -> p s r"), ALU.mult, ALU.mult)
            turned = psum.tile([P, 2, P], F32, name="w_turned%d" % h, tag="half%d" % h)
            turn_pairs(weights, turned)
            return turned

        V, S = nc.vector.tensor_copy, nc.scalar.copy
        vq, wq = {}, {}
        vt0 = gather_values(0)
        vt1 = gather_values(1)
        e0, e1 = exponentials()
        vq[0] = quantise_turned("val0", vt0, V, tag="sharp_sb")
        wt0 = turned_weights(0, *e0)
        wt1 = turned_weights(1, *e1)
        vq[1] = quantise_turned("val1", vt1, V, tag="largest", codes_tag="total1")
        vt2 = gather_values(2)
        w_grouped = sb("w_grouped", [P, Q, 2], F32)
        S(w_grouped[:, :P, :], wt0[:].rearrange("p u c -> p c u"))
        vt3 = gather_values(3)
        S(w_grouped[:, P:, :], wt1[:].rearrange("p u c -> p c u"))
        late_codes = sb("late_codes", [P, Q + P], U32, tag="val_pool3")
        w_codes = late_codes[:, :Q]
        w_scales = sb("w_scales", [P, Q], U8)
        nc.vector.quantize_mx(out=w_codes.bitcast(FP8X4), scales=w_scales[:],
                              in_=w_grouped[:].rearrange("p c u -> p (c u)").bitcast(BF16))
        vq[2] = quantise_turned("val2", vt2, S, codes=late_codes[:, Q:])

        out_planes = out_0.rearrange("(p t) q -> p t q", t=PACK)
        last = PACK - 1
        pair_sums = psum.tile([P, 2, Q], F32, name="pair_sums")
        sums = [pair_sums[:, 0, :], pair_sums[:, 1, :]] + [psum.tile([P, Q], F32, name="sums%d" % t)[:] for t in (2, 3)]

        def multiply(t):
            nc.tensor.matmul_mx(out=sums[t], lhsT=vq[t][0].bitcast(FP8X4), lhsT_scale=vq[t][1][:],
                                rhs=w_codes.bitcast(FP8X4), rhs_scale=w_scales[:], start=True, stop=True)

        y = sb("y", [P, PACK, Q], F32)
        for t in range(last):
            multiply(t)
        vq[last] = quantise_turned("val3", vt3, V)
        nc.scalar.copy(y[:, :2, :], pair_sums[:])
        nc.scalar.copy(y[:, 2, :], sums[2])
        nc.sync.dma_start(out_planes[:, :last, :], y[:, :last, :])
        multiply(last)
        nc.vector.tensor_copy(y[:, last, :], sums[last])
        nc.sync.dma_start(out_planes[:, last, :], y[:, last, :])

        y_bf = sb("y_bf", [P, Q, PACK], BF16)
        split = 160
        for copy, cols in ((V, slice(0, split)), (S, slice(split, Q))):
            copy(y_bf[:, cols, :].rearrange("p (c i) t -> p c t i", i=4), y[:, :, cols].rearrange("p t (c i) -> p c t i", i=4))
        y_codes = sb("y_codes", [P, Q], U32)
        y_scales = sb("y_scales", [P, Q], U8)
        nc.vector.quantize_mx(out=y_codes[:].bitcast(FP8X4), scales=y_scales[:], in_=y_bf[:].rearrange("p q t -> p (q t)"))
        nc.sync.dma_start(out_1[0].rearrange("p n t -> p (n t)").bitcast(I32), y_codes[:].bitcast(I32))
        out_rows = out_2[0].bitcast(I32)
        for quad in range(4):
            queue = nc.sync if quad < 2 else nc.scalar
            queue.dma_start(out_rows[4 * quad : 4 * quad + 4, :], y_scales[32 * quad : 32 * quad + 4, :].bitcast(I32))
